import numpy as np
import ml_dtypes


def mxq(x, axis, fmt="e4m3"):
    dtype, down = {"e4m3": (ml_dtypes.float8_e4m3fn, 7), "e5m2": (ml_dtypes.float8_e5m2, 14)}[fmt]
    v = np.moveaxis(np.asarray(x, np.float32).astype(ml_dtypes.bfloat16).astype(np.float64), axis, -1)
    blocks = v.reshape(v.shape[:-1] + (-1, 32))
    amax = np.abs(blocks).max(-1, keepdims=True)
    byte = np.maximum(np.where(amax > 0, np.frexp(amax)[1] - 1 + 127, 0) - down, 1)
    scale = np.exp2(byte - 127.0)
    codes = (blocks / scale).astype(np.float32).astype(dtype).astype(np.float64)
    return np.moveaxis((codes * scale).reshape(v.shape), -1, axis)


WIDE = False


def mx_kscale(k):
    if not WIDE:
        return np.ones(k)
    levels = np.array([10, -10, 5, -5, 0])
    if k % 512:
        return np.exp2(np.random.permutation(np.resize(levels, k // 32))).repeat(32)
    a = np.empty((k // 512, 16))
    for p in range(k // 512):
        a[p, :8] = np.random.permutation(np.resize(levels, 8))
        for g in range(8):
            far = levels[np.abs(levels - a[p, g]) >= 10]
            a[p, g + 8] = far[np.random.randint(len(far))]
    return np.exp2(a.ravel()).repeat(32)


BF16 = ml_dtypes.bfloat16


def bf(x):
    return np.asarray(x, np.float32).astype(BF16)


def f64(x):
    return np.asarray(x).astype(np.float64)


E2M1 = np.array([0.0, 0.5, 1.0, 1.5, 2.0, 3.0, 4.0, 6.0, -0.0, -0.5, -1.0, -1.5, -2.0, -3.0, -4.0, -6.0])


def pack_weight(w, fmt):
    k, n = w.shape
    w = f64(bf(w)).reshape(k // 32, 32, n)
    amax = np.abs(w).max(1)
    if fmt == "e4m3":
        byte = np.frexp(amax)[1] - 1 + 127 - 7
    else:
        mant, ex = np.frexp(amax / 6.0)
        byte = np.where(mant > 0.5, ex, ex - 1) + 127
    byte = np.clip(np.where(amax > 0, byte, 1), 1, 254)
    scaled = (w * np.exp2(127.0 - byte)[:, None, :]).reshape(k, n).astype(np.float32)
    by_word = np.ascontiguousarray(scaled.reshape(k // 512, 128, 4, n).transpose(0, 1, 3, 2))
    if fmt == "e4m3":
        words = by_word.astype(ml_dtypes.float8_e4m3fn).view(np.uint8)
    else:
        c = by_word.astype(ml_dtypes.float4_e2m1fn).view(np.uint8) & 0xF
        words = c[..., 0::2] | (c[..., 1::2] << 4)
    return np.ascontiguousarray(words), np.ascontiguousarray(byte.astype(np.uint8).reshape(k // 512, 16, n))


def unpack_weight(words, scales, fmt):
    g, p, n, _ = words.shape
    if fmt == "e4m3":
        vals = np.ascontiguousarray(words).view(ml_dtypes.float8_e4m3fn).astype(np.float64)
    else:
        nib = np.empty((g, p, n, 4), np.uint8)
        nib[..., 0::2] = words & 0xF
        nib[..., 1::2] = words >> 4
        vals = E2M1[nib]
    vals = vals * np.repeat(np.exp2(scales.astype(np.float64) - 127.0), 8, axis=1)[..., None]
    return vals.transpose(0, 1, 3, 2).reshape(g * 512, n)
def pack4(w):
    words, scales = pack_weight(w, "e2m1")
    return words.reshape(words.shape[0], 128, -1), scales


def unpack4(words, scales):
    return unpack_weight(words.reshape(words.shape[0], 128, -1, 2), scales, "e2m1")


def planes(Y):
    n, m = Y.shape
    b = f64(bf(Y)).reshape(n // 32, 32, m)
    amax = np.abs(b).max(1)
    byte = np.clip(np.where(amax > 0, np.frexp(amax)[1] - 1 + 127 - 7, 1), 1, 254)
    codes = (b * np.exp2(127.0 - byte)[:, None, :]).reshape(n, m).astype(np.float32).astype(ml_dtypes.float8_e4m3fn).view(np.uint8)
    words = codes.reshape(n // 512, 128, 4, m).transpose(0, 1, 3, 2)
    return np.ascontiguousarray(words), np.ascontiguousarray(byte.astype(np.uint8).reshape(n // 512, 16, m))


M, D, E, R, N = 1024, 1536, 16, 512, 2048
RANK = R // E


def setup_inputs():
    rn = np.random.randn
    s = mx_kscale(D)
    t = mx_kscale(R)
    x = rn(M, D) * s
    down = rn(D, R) / np.sqrt(D) / s[:, None] * t
    up = 0.25 * rn(R, D) / np.sqrt(R) / t[:, None] * s
    gates = np.repeat(np.exp(0.5 * rn(M, E)), RANK, axis=1) * np.exp(0.3 * rn(M, R))
    w = rn(D, N) / np.sqrt(D) / s[:, None]
    w_words, w_scales = pack4(w)
    return {"x": bf(x), "down": bf(down), "gates": bf(gates), "up": bf(up),
            "w_words": w_words, "w_scales": w_scales,
            "bias": bf(0.4 * rn(N)), "gain": bf(np.exp(0.8 * rn(N)))}


def reference(x, down, gates, up, w_words, w_scales, bias, gain):
    xf = f64(x)
    z = mxq(xf, 1) @ mxq(f64(down), 0)
    h = z * f64(gates)
    u = mxq(h, 1) @ mxq(f64(up), 0)
    x1 = xf + u
    v = (mxq(x1, 1) @ unpack4(w_words, w_scales)) + f64(bias)
    y = v / (1.0 + np.exp(-v)) * f64(gain)
    words, scales = planes(y.T)
    return y, words, scales

@@ -1,0 +1,431 @@
+from contextlib import ExitStack
+
+import concourse.mybir as mybir
+from concourse.masks import make_identity
+
+M, D, R, N = 1024, 1536, 512, 2048
+FLOPS = 2 * M * (D * R + R * D + D * N)
+
+F32 = mybir.dt.float32
+BF16 = mybir.dt.bfloat16
+I32 = mybir.dt.int32
+U32 = mybir.dt.uint32
+U8 = mybir.dt.uint8
+FP8X4 = mybir.dt.float8_e4m3fn_x4
+FP4X4 = mybir.dt.float4_e2m1fn_x4
+ALU = mybir.AluOpType
+ACT = mybir.ActivationFunctionType
+
+P = 128
+PACK = 4
+KP = P * PACK
+DG = D // KP
+NG = N // KP
+PAIR = 2 * P
+HALF = 4 * P
+DOWN_ON = 'vvv'
+UP_ON = 'sss'
+LAG = 4
+WIDE = 8
+GAIN_ON = 'sssvvvvv'
+COPY_ON = ['ssss'] * 7 + ['svsv']
+TURN_AT = 3
+PLANES_AT = {0: 14, 1: 17, 2: 19, 3: 21, 4: 23, 5: 26, 6: 29}
+
+
+def tile_gated_lowrank_experts_projection_k1_kernel(
+    tc, x, down, gates, up, w_words, w_scales, bias, gain, out_0, out_1, out_2
+):
+    nc = tc.nc
+    with ExitStack() as ctx:
+        keep = ctx.enter_context(tc.tile_pool(name="keep", bufs=1))
+        psum = ctx.enter_context(tc.psum_pool(name="psum", bufs=1))
+        ctx.enter_context(tc.manual_schedule())
+
+        def kept(name, shape, dtype):
+            return keep.tile(shape, dtype, name=name, align_bytes=64)
+
+        def ring(tag, bufs, shape, dtype):
+            return keep.tile(shape, dtype, name=tag, tag=tag, bufs=bufs, align_bytes=64)
+
+        free_banks = list(range(8))
+
+        def take_bank():
+            b = free_banks.pop(0)
+            bank = psum.tile([P, PACK, P], F32, name="bank%d" % b, tag="bank%d" % b)
+            return b, bank
+
+        def quantize(codes, scales, src):
+            nc.vector.quantize_mx(out=codes.bitcast(FP8X4), scales=scales, in_=src)
+
+        ident = kept("ident", [P, P], F32)
+        make_identity(nc, ident[:])
+        ws_raw = kept("ws_raw", [P, DG, N], U8)
+        nc.gpsimd.memset(ws_raw[:].rearrange("p g n -> p (g n)").bitcast(I32), 0)
+        warm = kept("warm", [P, 2], F32)
+        nc.vector.memset(warm[:, 0:1], 0.0)
+        nc.scalar.activation(out=warm[:, 1:2], in_=warm[:, 0:1], func=ACT.Silu)
+        bias_sb = kept("bias_sb", [P, NG, PACK], BF16)
+        gain_sb = kept("gain_sb", [P, NG, PACK], BF16)
+
+        x_raw, g_raw, down_raw, up_raw, w_raw = {}, {}, {}, {}, {}
+
+        def wide(shape, dtype):
+            return ring("wide", WIDE, shape, dtype)
+
+        def load_x(pr):
+            x_raw[pr] = wide([P, 2, D], BF16)
+            for i in range(2):
+                r0 = pr * PAIR + i * P
+                nc.sync.dma_start(out=x_raw[pr][:, i, :], in_=x[r0 : r0 + P, :])
+
+        def load_gates(pr):
+            g_raw[pr] = ring("g_raw", 3, [P, 2, R], BF16)
+            rows = gates[pr * PAIR : (pr + 1) * PAIR, :]
+            nc.sync.dma_start(out=g_raw[pr][:], in_=rows.rearrange("(i p) r -> p i r", p=P))
+
+        def load_down(g):
+            down_raw[g] = wide([P, PACK, KP], BF16)
+            rows = down[g * KP : (g + 1) * KP, :]
+            nc.sync.dma_start(out=down_raw[g][:], in_=rows.rearrange("(p j) c -> p j c", j=PACK))
+
+        def load_up(g):
+            up_raw[g] = wide([P, PACK, KP], BF16)
+            cols = up[:, g * KP : (g + 1) * KP]
+            nc.sync.dma_start(out=up_raw[g][:], in_=cols.rearrange("(p j) c -> p j c", j=PACK))
+
+        def load_w(n):
+            w_raw[n] = ring("w_raw", 4, [P, DG, 2 * KP], U8)
+            src = w_words[:, :, 2 * KP * n : 2 * KP * (n + 1)].rearrange("g p b -> p g b")
+            nc.sync.dma_start(out=w_raw[n][:].bitcast(I32), in_=src.bitcast(I32))
+
+        def load_w_scales():
+            for q in range(4):
+                src = w_scales[:, 4 * q : 4 * q + 4, :].rearrange("g r n -> r g n")
+                nc.sync.dma_start(out=ws_raw[32 * q : 32 * q + 4, :, :].bitcast(I32), in_=src.bitcast(I32))
+
+        def load_vectors():
+            nc.sync.dma_start(out=bias_sb[:], in_=bias.rearrange("(g p t) -> p g t", p=P, t=PACK))
+            nc.sync.dma_start(out=gain_sb[:], in_=gain.rearrange("(g p t) -> p g t", p=P, t=PACK))
+
+        gain_f32 = kept("gain_f32", [P, NG, PACK], F32)
+
+        xt, xq, xs, gt = {}, {}, {}, {}
+        dq, ds, uq, us, grouped = {}, {}, {}, {}, {}
+        hb, hq, hs = {}, {}, {}
+        x1q, x1s = {}, {}
+        wq, ws = {}, {}
+
+        def turn(raws, g, dst):
+            b, bank = take_bank()
+            for i in range(2):
+                words = raws[i].bitcast(F32)
+                for u in range(2):
+                    nc.tensor.transpose(bank[:, 2 * i + u, :], words[:, 256 * g + u : 256 * (g + 1) : 2], ident[:])
+            nc.scalar.copy(
+                out=dst.bitcast(F32).rearrange("p (i r u) -> p i r u", i=2, u=2),
+                in_=bank[:].rearrange("p (i u) r -> p i r u", u=2),
+            )
+            free_banks.append(b)
+
+        def turn_x(pr, g):
+            h = pr // 2
+            if (h, g) not in xt:
+                xt[h, g] = kept("xt%d_%d" % (h, g), [P, 2, PAIR * PACK], BF16)
+            turn([x_raw[pr][:, 0, :], x_raw[pr][:, 1, :]], g, xt[h, g][:, pr % 2, :])
+
+        def turn_gates(pr):
+            gt[pr] = ring("gt", 4, [P, PAIR * PACK], BF16)
+            turn([g_raw[pr][:, 0, :], g_raw[pr][:, 1, :]], 0, gt[pr][:])
+
+        def quantize_x(pr, g):
+            xq[pr, g] = ring("xq", 9, [P, PAIR], U32)
+            xs[pr, g] = ring("xs", 9, [P, PAIR], U8)
+            quantize(xq[pr, g][:], xs[pr, g][:], xt[pr // 2, g][:, pr % 2, :])
+
+        def group_factor(key, raw, engine):
+            grouped[key] = ring("grouped", 3, [P, KP * PACK], BF16)
+            dst = grouped[key][:].rearrange("p (t m j) -> p t m j", t=PACK, j=PACK)
+            src = raw[:].rearrange("p j (m t) -> p t m j", t=PACK)
+            if engine == "v":
+                nc.vector.tensor_copy(out=dst, in_=src)
+            else:
+                nc.scalar.copy(out=dst, in_=src)
+
+        def quantize_factor(key, codes, scales):
+            codes[key[1]] = kept("%s_q%d" % key, [P, KP], U32)
+            scales[key[1]] = kept("%s_s%d" % key, [P, KP], U8)
+            quantize(codes[key[1]][:], scales[key[1]][:], grouped[key][:])
+
+        def order_w_codes(n, g):
+            wq[n, g] = kept("wq%d_%d" % (n, g), [P, 2 * KP], U8)
+            nc.vector.tensor_copy(
+                out=wq[n, g][:].rearrange("p (t m b) -> p t m b", t=PACK, b=2),
+                in_=w_raw[n][:, g, :].rearrange("p (m t b) -> p t m b", t=PACK, b=2),
+            )
+
+        def order_w_scales(n):
+            ws[n] = kept("ws%d" % n, [P, DG, KP], U8)
+            nc.vector.tensor_copy(
+                out=ws[n][:].rearrange("p g (t m) -> p g t m", t=PACK),
+                in_=ws_raw[:, :, n * KP : (n + 1) * KP].rearrange("p g (m t) -> p g t m", t=PACK),
+            )
+
+        def stage1(i):
+            pr = i // 2
+            tok = slice((i % 2) * P, (i % 2 + 1) * P)
+            b, bank = take_bank()
+            for t in range(PACK):
+                col = slice(t * P, (t + 1) * P)
+                for g in range(DG):
+                    nc.tensor.matmul_mx(
+                        out=bank[:, t, :], lhsT=dq[g][:, col].bitcast(FP8X4), lhsT_scale=ds[g][:, col],
+                        rhs=xq[pr, g][:, tok].bitcast(FP8X4), rhs_scale=xs[pr, g][:, tok],
+                        start=(g == 0), stop=(g == DG - 1),
+                    )
+            if pr not in hb:
+                hb[pr] = ring("hb", 2, [P, PAIR * PACK], BF16)
+            span = slice((i % 2) * KP, (i % 2 + 1) * KP)
+            nc.vector.tensor_tensor(
+                out=hb[pr][:, span].rearrange("p (r t) -> p r t", t=PACK),
+                in0=bank[:].rearrange("p t r -> p r t"),
+                in1=gt[pr][:, span].rearrange("p (r t) -> p r t", t=PACK),
+                op=ALU.mult,
+            )
+            free_banks.append(b)
+
+        def quantize_h(pr):
+            hq[pr] = ring("hq", 2, [P, PAIR], U32)
+            hs[pr] = ring("hs", 2, [P, PAIR], U8)
+            quantize(hq[pr][:], hs[pr][:], hb[pr][:])
+
+        def stage2(i, g):
+            pr = i // 2
+            tok = slice((i % 2) * P, (i % 2 + 1) * P)
+            b, bank = take_bank()
+            for t in range(PACK):
+                col = slice(t * P, (t + 1) * P)
+                nc.tensor.matmul_mx(
+                    out=bank[:, t, :], lhsT=uq[g][:, col].bitcast(FP8X4), lhsT_scale=us[g][:, col],
+                    rhs=hq[pr][:, tok].bitcast(FP8X4), rhs_scale=hs[pr][:, tok], start=True, stop=True,
+                )
+            span = slice((i % 2) * KP, (i % 2 + 1) * KP)
+            x_part = xt[i // 4, g][:, pr % 2, span].rearrange("p (r t) -> p r t", t=PACK)
+            nc.vector.tensor_tensor(out=x_part, in0=bank[:].rearrange("p t r -> p r t"), in1=x_part, op=ALU.add)
+            free_banks.append(b)
+
+        def quantize_x1(h, g):
+            x1q[h, g] = kept("x1q%d_%d" % (h, g), [P, HALF], U32)
+            x1s[h, g] = kept("x1s%d_%d" % (h, g), [P, HALF], U8)
+            quantize(x1q[h, g][:], x1s[h, g][:], xt[h, g][:].rearrange("p i c -> p (i c)"))
+
+        yt, acc, yb = {}, {}, {}
+        y_scales = [kept("y_scales%d" % h, [P, NG, HALF], U8) for h in range(2)]
+
+        def stage3_pass(k, t, g):
+            h, n = divmod(k, NG)
+            if g == 0:
+                acc[k, t] = take_bank()
+            nc.tensor.matmul_mx(
+                out=acc[k, t][1][:].rearrange("p a b -> p (a b)"),
+                lhsT=wq[n, g][:, 2 * P * t : 2 * P * (t + 1)].bitcast(FP4X4),
+                lhsT_scale=ws[n][:, g, P * t : P * (t + 1)],
+                rhs=x1q[h, g][:].bitcast(FP8X4), rhs_scale=x1s[h, g][:],
+                start=(g == 0), stop=(g == DG - 1),
+            )
+
+        def silu(k, t):
+            n = k % NG
+            if t == 0:
+                yt[k] = wide([P, PACK, HALF], F32)
+            b, bank = acc[k, t]
+            nc.scalar.activation(
+                out=yt[k][:, t, :], in_=bank[:].rearrange("p a b -> p (a b)"), func=ACT.Silu,
+                bias=bias_sb[:, n, t : t + 1],
+            )
+            free_banks.append(b)
+
+        def apply_gain(k, t):
+            factor = gain_f32[:, k % NG, t : t + 1]
+            if GAIN_ON[k] == "v":
+                nc.vector.tensor_scalar(
+                    out=yt[k][:, t, :], in0=yt[k][:, t, :], scalar1=factor, scalar2=None, op0=ALU.mult
+                )
+            else:
+                nc.scalar.activation(out=yt[k][:, t, :], in_=yt[k][:, t, :], func=ACT.Copy, scale=factor)
+
+        def turn_y(k, on):
+            h, n = divmod(k, NG)
+            banks = []
+            for i in range(4):
+                b, bank = take_bank()
+                banks.append((b, bank))
+                for t in range(PACK):
+                    nc.tensor.transpose(bank[:, t, :], yt[k][:, t, i * P : (i + 1) * P], ident[:])
+            for i in range(4):
+                b, bank = banks[i]
+                rows = ring("y_rows", 8, [P, KP], F32)
+                dst = rows[:].rearrange("r (p t) -> r p t", t=PACK)
+                src = bank[:].rearrange("r t p -> r p t")
+                if on[i] == "v":
+                    nc.vector.tensor_copy(out=dst, in_=src)
+                else:
+                    nc.scalar.copy(out=dst, in_=src)
+                free_banks.append(b)
+                r0 = h * HALF + i * P
+                nc.sync.dma_start(out=out_0[r0 : r0 + P, n * KP : (n + 1) * KP], in_=rows[:])
+
+        def group_y(k):
+            yb[k] = ring("yb", 2, [P, HALF * PACK], BF16)
+            nc.vector.tensor_copy(
+                out=yb[k][:].rearrange("p (r t) -> p r t", t=PACK), in_=yt[k][:].rearrange("p t r -> p r t")
+            )
+
+        def quantize_y(k):
+            h, n = divmod(k, NG)
+            codes = ring("y_codes", 3, [P, HALF], U32)
+            quantize(codes[:], y_scales[h][:, n, :], yb[k][:])
+            dst = out_1[n, :, h * HALF : (h + 1) * HALF, :].rearrange("p m t -> p (m t)")
+            nc.sync.dma_start(out=dst.bitcast(I32), in_=codes[:].bitcast(I32))
+
+        def store_y_scales(h, n0, n1):
+            tok = slice(h * HALF, (h + 1) * HALF)
+            for q in range(4):
+                dst = out_2[n0:n1, 4 * q : 4 * q + 4, tok].rearrange("g r m -> r g m")
+                nc.sync.dma_start(out=dst.bitcast(I32), in_=y_scales[h][32 * q : 32 * q + 4, n0:n1, :].bitcast(I32))
+
+        load_down(0)
+        load_x(0)
+        load_down(1)
+        load_down(2)
+        load_gates(0)
+        load_up(0)
+        load_x(1)
+        load_gates(1)
+        load_up(1)
+        load_up(2)
+        load_w_scales()
+        load_w(0)
+        load_vectors()
+
+        group_factor(("down", 0), down_raw[0], DOWN_ON[0])
+        load_x(2)
+        load_gates(2)
+        for g in range(DG):
+            turn_x(0, g)
+        turn_gates(0)
+        quantize_factor(("down", 0), dq, ds)
+        group_factor(("down", 1), down_raw[1], DOWN_ON[1])
+        quantize_x(0, 0)
+        group_factor(("down", 2), down_raw[2], DOWN_ON[2])
+        load_w(1)
+        load_x(3)
+        load_gates(3)
+        load_w(2)
+        load_w(3)
+        quantize_factor(("down", 1), dq, ds)
+        quantize_x(0, 1)
+        quantize_x(0, 2)
+        quantize_factor(("down", 2), dq, ds)
+        group_factor(("up", 0), up_raw[0], UP_ON[0])
+        stage1(0)
+        stage1(1)
+        for g in range(DG):
+            turn_x(1, g)
+        turn_gates(1)
+        quantize_factor(("up", 0), uq, us)
+        quantize_h(0)
+        for g in range(DG):
+            quantize_x(1, g)
+        group_factor(("up", 1), up_raw[1], UP_ON[1])
+        stage2(0, 0)
+        stage2(1, 0)
+        stage1(2)
+        stage1(3)
+        group_factor(("up", 2), up_raw[2], UP_ON[2])
+        nc.scalar.copy(out=gain_f32[:], in_=gain_sb[:])
+        quantize_factor(("up", 1), uq, us)
+        quantize_h(1)
+        stage2(0, 1)
+        stage2(1, 1)
+        stage2(2, 0)
+        stage2(3, 0)
+        for g in range(DG):
+            turn_x(2, g)
+        turn_gates(2)
+        order_w_scales(0)
+        quantize_x1(0, 0)
+        stage2(2, 1)
+        stage2(3, 1)
+        quantize_factor(("up", 2), uq, us)
+        order_w_codes(0, 0)
+        quantize_x1(0, 1)
+        for g in range(DG):
+            turn_x(3, g)
+        turn_gates(3)
+        stage2(0, 2)
+        order_w_codes(0, 1)
+        for i in range(1, 4):
+            stage2(i, 2)
+        for g in range(2):
+            for t in range(PACK):
+                stage3_pass(0, t, g)
+        order_w_codes(0, 2)
+        quantize_x1(0, 2)
+
+        extra = {}
+
+        def later(s, *job):
+            extra.setdefault(s, []).append(job)
+
+        for g in range(DG):
+            later(0, quantize_x, 2, g)
+        later(0, stage1, 4)
+        later(1, order_w_scales, 1)
+        later(1, stage1, 5)
+        for g in range(DG):
+            later(1 + g, order_w_codes, 1, g)
+        for n in range(2, NG):
+            later(4 * n - 4, order_w_scales, n)
+            for g in range(DG):
+                later(4 * n - 4 + g, order_w_codes, n, g)
+        for g in range(DG):
+            later(3, quantize_x, 3, g)
+        later(4, stage1, 6)
+        later(2, quantize_h, 2)
+        later(5, stage1, 7)
+        later(6, stage2, 4, 0)
+        later(6, quantize_h, 3)
+        slots = {(5, 0): 7, (6, 0): 7, (7, 0): 8, (4, 1): 9, (5, 1): 10, (6, 1): 11, (7, 1): 11,
+                 (4, 2): 12, (5, 2): 12, (6, 2): 13, (7, 2): 13}
+        for (i, g), s in slots.items():
+            later(s, stage2, i, g)
+            if i == 7:
+                later(s + 1, quantize_x1, 1, g)
+        units = 2 * NG
+        planes_at = PLANES_AT
+        for k, s in planes_at.items():
+            later(s, group_y, k)
+            later(s + 1, quantize_y, k)
+        later(planes_at[3] + 2, store_y_scales, 0, 0, NG)
+        later(planes_at[6] + 2, store_y_scales, 1, 0, NG - 1)
+
+        for k in range(units):
+            for t in range(PACK):
+                for g in range(DG):
+                    if k > 0 or g == DG - 1:
+                        stage3_pass(k, t, g)
+                silu(k, t)
+                if t > 0:
+                    apply_gain(k, t - 1)
+                elif k > 0:
+                    apply_gain(k - 1, PACK - 1)
+                for job in extra.get(PACK * k + t, []):
+                    job[0](*job[1:])
+                if k > 0 and t == TURN_AT:
+                    turn_y(k - 1, COPY_ON[k - 1])
+        apply_gain(units - 1, PACK - 1)
+        group_y(units - 1)
+        quantize_y(units - 1)
+        turn_y(units - 1, COPY_ON[units - 1])
+        store_y_scales(1, NG - 1, NG)

@@ -23,14 +23,450 @@ DG = D // KP
 NG = N // KP
 PAIR = 2 * P
 HALF = 4 * P
-DOWN_ON = 'vvv'
-UP_ON = 'sss'
-LAG = 4
 WIDE = 8
-GAIN_ON = 'sssvvvvv'
-COPY_ON = ['ssss'] * 7 + ['svsv']
-TURN_AT = 3
-PLANES_AT = {0: 14, 1: 17, 2: 19, 3: 21, 4: 23, 5: 26, 6: 29}
+ORDER = [
+    ('ld', 0),
+    ('gf', 'down', 0, 0, 'v'),
+    ('gf', 'down', 0, 1, 's'),
+    ('ld', 1),
+    ('lx', 0, 0),
+    ('lx', 0, 1),
+    ('ld', 2),
+    ('gf', 'down', 1, 0, 'v'),
+    ('lx', 1, 0),
+    ('lx', 1, 1),
+    ('lr',),
+    ('tx', 0, 0),
+    ('cx', 0, 0),
+    ('gf', 'down', 1, 1, 'v'),
+    ('tx', 0, 1),
+    ('cx', 0, 1),
+    ('lg', 0),
+    ('lw', 0),
+    ('tx', 0, 2),
+    ('cx', 0, 2),
+    ('qf', 'down', 0),
+    ('tx', 1, 0),
+    ('cx', 1, 0),
+    ('tx', 1, 1),
+    ('cx', 1, 1),
+    ('lu', 0),
+    ('qf', 'down', 1),
+    ('tx', 1, 2),
+    ('cx', 1, 2),
+    ('gf', 'down', 2, 0, 'v'),
+    ('tg', 0),
+    ('cg', 0),
+    ('gf', 'down', 2, 1, 'v'),
+    ('lg', 1),
+    ('qx', 0, 0),
+    ('qf', 'down', 2),
+    ('qx', 0, 1),
+    ('qx', 0, 2),
+    ('ws',),
+    ('gf', 'up', 0, 2, 's'),
+    ('qx', 1, 0),
+    ('wc', 0, 0),
+    ('qx', 1, 1),
+    ('wc', 0, 1),
+    ('qx', 1, 2),
+    ('s1', 0),
+    ('h', 0),
+    ('lx', 2, 0),
+    ('lu', 1),
+    ('s1', 1),
+    ('h', 1),
+    ('lg', 2),
+    ('wc', 0, 2),
+    ('tg', 1),
+    ('cg', 1),
+    ('gf', 'up', 1, 2, 's'),
+    ('qh', 0),
+    ('lx', 2, 1),
+    ('qf', 'up', 0),
+    ('s1', 2),
+    ('h', 2),
+    ('s1', 3),
+    ('h', 3),
+    ('s2', 0, 0),
+    ('x1', 0, 0),
+    ('lu', 2),
+    ('tg', 2),
+    ('cg', 2),
+    ('qh', 1),
+    ('s2', 1, 0),
+    ('x1', 1, 0),
+    ('gf', 'up', 2, 2, 's'),
+    ('qf', 'up', 1),
+    ('tx', 2, 0),
+    ('cx', 2, 0),
+    ('s2', 2, 0),
+    ('x1', 2, 0),
+    ('s2', 3, 0),
+    ('x1', 3, 0),
+    ('s2', 0, 1),
+    ('x1', 0, 1),
+    ('lg', 3),
+    ('s2', 1, 1),
+    ('x1', 1, 1),
+    ('tx', 2, 1),
+    ('cx', 2, 1),
+    ('tx', 2, 2),
+    ('cx', 2, 2),
+    ('qf', 'up', 2),
+    ('q1', 0, 0),
+    ('tg', 3),
+    ('cg', 3),
+    ('ls',),
+    ('s2', 2, 1),
+    ('x1', 2, 1),
+    ('s2', 3, 1),
+    ('x1', 3, 1),
+    ('lx', 3, 0),
+    ('s2', 0, 2),
+    ('x1', 0, 2),
+    ('s2', 1, 2),
+    ('x1', 1, 2),
+    ('s2', 2, 2),
+    ('x1', 2, 2),
+    ('q1', 0, 1),
+    ('s3', 0, 0, 0),
+    ('s3', 0, 1, 0),
+    ('s2', 3, 2),
+    ('x1', 3, 2),
+    ('q1', 0, 2),
+    ('qx', 2, 0),
+    ('s3', 0, 2, 0),
+    ('lx', 3, 1),
+    ('s3', 0, 3, 0),
+    ('tx', 3, 0),
+    ('cx', 3, 0),
+    ('tx', 3, 1),
+    ('cx', 3, 1),
+    ('qx', 2, 1),
+    ('tx', 3, 2),
+    ('cx', 3, 2),
+    ('lw', 1),
+    ('s3', 0, 0, 1),
+    ('s3', 0, 1, 1),
+    ('lv',),
+    ('lw', 2),
+    ('qx', 2, 2),
+    ('s3', 0, 2, 1),
+    ('s3', 0, 3, 1),
+    ('qx', 3, 0),
+    ('wg',),
+    ('s3', 0, 0, 2),
+    ('si', 0, 0),
+    ('wc', 1, 0),
+    ('wc', 1, 1),
+    ('wc', 1, 2),
+    ('s3', 0, 1, 2),
+    ('si', 0, 1),
+    ('qx', 3, 1),
+    ('qx', 3, 2),
+    ('s3', 0, 2, 2),
+    ('si', 0, 2),
+    ('ga', 0, 0, 's'),
+    ('ga', 0, 1, 's'),
+    ('s1', 4),
+    ('h', 4),
+    ('lw', 3),
+    ('s3', 0, 3, 2),
+    ('si', 0, 3),
+    ('s1', 5),
+    ('h', 5),
+    ('s3', 1, 0, 0),
+    ('s3', 1, 0, 1),
+    ('s3', 1, 0, 2),
+    ('si', 1, 0),
+    ('ga', 0, 2, 's'),
+    ('ga', 0, 3, 's'),
+    ('wc', 2, 0),
+    ('wc', 2, 1),
+    ('qh', 2),
+    ('s3', 1, 1, 0),
+    ('s3', 1, 1, 1),
+    ('s3', 1, 1, 2),
+    ('si', 1, 1),
+    ('wc', 2, 2),
+    ('s3', 1, 2, 0),
+    ('s3', 1, 2, 1),
+    ('s3', 1, 2, 2),
+    ('si', 1, 2),
+    ('ga', 1, 0, 'v'),
+    ('ga', 1, 1, 'v'),
+    ('ga', 1, 2, 'v'),
+    ('gy', 0, 2, 's'),
+    ('s1', 6),
+    ('h', 6),
+    ('s1', 7),
+    ('h', 7),
+    ('s2', 4, 0),
+    ('x1', 4, 0),
+    ('qh', 3),
+    ('s3', 1, 3, 0),
+    ('s3', 1, 3, 1),
+    ('s3', 1, 3, 2),
+    ('si', 1, 3),
+    ('s3', 2, 0, 0),
+    ('s3', 2, 0, 1),
+    ('s3', 2, 0, 2),
+    ('si', 2, 0),
+    ('ga', 1, 3, 's'),
+    ('qy', 0),
+    ('sc', 0),
+    ('s2', 5, 0),
+    ('x1', 5, 0),
+    ('s2', 4, 1),
+    ('x1', 4, 1),
+    ('s3', 2, 1, 0),
+    ('s3', 2, 1, 1),
+    ('s3', 2, 1, 2),
+    ('si', 2, 1),
+    ('ga', 2, 0, 's'),
+    ('ga', 2, 1, 's'),
+    ('s2', 6, 0),
+    ('x1', 6, 0),
+    ('s2', 7, 0),
+    ('x1', 7, 0),
+    ('s2', 5, 1),
+    ('x1', 5, 1),
+    ('s2', 6, 1),
+    ('x1', 6, 1),
+    ('s3', 2, 2, 0),
+    ('s3', 2, 2, 1),
+    ('s3', 2, 2, 2),
+    ('si', 2, 2),
+    ('ty', 0, 0),
+    ('ty', 0, 1),
+    ('cy', 0, 0, 's'),
+    ('cy', 0, 1, 'v'),
+    ('sy', 0, 0, 2),
+    ('ty', 0, 2),
+    ('ty', 0, 3),
+    ('cy', 0, 2, 's'),
+    ('cy', 0, 3, 's'),
+    ('sy', 0, 2, 4),
+    ('ty', 1, 0),
+    ('ty', 1, 1),
+    ('cy', 1, 0, 's'),
+    ('cy', 1, 1, 's'),
+    ('sy', 1, 0, 2),
+    ('ty', 1, 2),
+    ('ty', 1, 3),
+    ('cy', 1, 2, 's'),
+    ('cy', 1, 3, 's'),
+    ('sy', 1, 2, 4),
+    ('wc', 3, 0),
+    ('wc', 3, 1),
+    ('wc', 3, 2),
+    ('s2', 7, 1),
+    ('x1', 7, 1),
+    ('s2', 4, 2),
+    ('x1', 4, 2),
+    ('s2', 5, 2),
+    ('x1', 5, 2),
+    ('s2', 6, 2),
+    ('x1', 6, 2),
+    ('s2', 7, 2),
+    ('x1', 7, 2),
+    ('s3', 2, 3, 0),
+    ('s3', 2, 3, 1),
+    ('s3', 2, 3, 2),
+    ('si', 2, 3),
+    ('q1', 1, 0),
+    ('s3', 3, 0, 0),
+    ('s3', 3, 0, 1),
+    ('s3', 3, 0, 2),
+    ('si', 3, 0),
+    ('ga', 2, 2, 'v'),
+    ('ga', 2, 3, 's'),
+    ('ga', 3, 0, 's'),
+    ('q1', 1, 1),
+    ('q1', 1, 2),
+    ('s3', 3, 1, 0),
+    ('s3', 3, 1, 1),
+    ('s3', 3, 1, 2),
+    ('si', 3, 1),
+    ('gy', 1, 2, 'v'),
+    ('s3', 3, 2, 0),
+    ('s3', 3, 2, 1),
+    ('s3', 3, 2, 2),
+    ('si', 3, 2),
+    ('s3', 3, 3, 0),
+    ('s3', 3, 3, 1),
+    ('s3', 3, 3, 2),
+    ('si', 3, 3),
+    ('ga', 3, 1, 's'),
+    ('s3', 4, 0, 0),
+    ('s3', 4, 0, 1),
+    ('s3', 4, 0, 2),
+    ('si', 4, 0),
+    ('ga', 3, 2, 'v'),
+    ('ga', 3, 3, 'v'),
+    ('qy', 1),
+    ('sc', 1),
+    ('s3', 4, 1, 0),
+    ('s3', 4, 1, 1),
+    ('s3', 4, 1, 2),
+    ('si', 4, 1),
+    ('ga', 4, 0, 's'),
+    ('ty', 2, 0),
+    ('ty', 2, 1),
+    ('cy', 2, 0, 's'),
+    ('cy', 2, 1, 'v'),
+    ('sy', 2, 0, 2),
+    ('ty', 2, 2),
+    ('ty', 2, 3),
+    ('cy', 2, 2, 'v'),
+    ('cy', 2, 3, 's'),
+    ('sy', 2, 2, 4),
+    ('ty', 3, 0),
+    ('ty', 3, 1),
+    ('cy', 3, 0, 'v'),
+    ('cy', 3, 1, 's'),
+    ('sy', 3, 0, 2),
+    ('gy', 2, 2, 'v'),
+    ('gy', 3, 2, 'v'),
+    ('qy', 2),
+    ('sc', 2),
+    ('s3', 4, 2, 0),
+    ('s3', 4, 2, 1),
+    ('s3', 4, 2, 2),
+    ('si', 4, 2),
+    ('s3', 4, 3, 0),
+    ('s3', 4, 3, 1),
+    ('s3', 4, 3, 2),
+    ('si', 4, 3),
+    ('ga', 4, 1, 's'),
+    ('s3', 5, 0, 0),
+    ('s3', 5, 0, 1),
+    ('s3', 5, 0, 2),
+    ('si', 5, 0),
+    ('ga', 4, 2, 'v'),
+    ('ga', 4, 3, 'v'),
+    ('ga', 5, 0, 'v'),
+    ('s3', 5, 1, 0),
+    ('s3', 5, 1, 1),
+    ('s3', 5, 1, 2),
+    ('si', 5, 1),
+    ('qy', 3),
+    ('sc', 3),
+    ('s3', 5, 2, 0),
+    ('s3', 5, 2, 1),
+    ('s3', 5, 2, 2),
+    ('si', 5, 2),
+    ('ga', 5, 1, 'v'),
+    ('ss', 0),
+    ('s3', 5, 3, 0),
+    ('s3', 5, 3, 1),
+    ('s3', 5, 3, 2),
+    ('si', 5, 3),
+    ('ga', 5, 2, 'v'),
+    ('ga', 5, 3, 'v'),
+    ('ty', 3, 2),
+    ('ty', 3, 3),
+    ('cy', 3, 2, 'v'),
+    ('cy', 3, 3, 's'),
+    ('sy', 3, 2, 4),
+    ('ty', 4, 0),
+    ('ty', 4, 1),
+    ('cy', 4, 0, 's'),
+    ('cy', 4, 1, 's'),
+    ('sy', 4, 0, 2),
+    ('ty', 4, 2),
+    ('ty', 4, 3),
+    ('cy', 4, 2, 'v'),
+    ('cy', 4, 3, 'v'),
+    ('sy', 4, 2, 4),
+    ('ty', 5, 0),
+    ('ty', 5, 1),
+    ('cy', 5, 0, 's'),
+    ('cy', 5, 1, 's'),
+    ('sy', 5, 0, 2),
+    ('gy', 4, 2, 'v'),
+    ('s3', 6, 0, 0),
+    ('s3', 6, 0, 1),
+    ('s3', 6, 0, 2),
+    ('si', 6, 0),
+    ('gy', 5, 2, 'v'),
+    ('qy', 4),
+    ('sc', 4),
+    ('s3', 6, 1, 0),
+    ('s3', 6, 1, 1),
+    ('s3', 6, 1, 2),
+    ('si', 6, 1),
+    ('s3', 6, 2, 0),
+    ('s3', 6, 2, 1),
+    ('s3', 6, 2, 2),
+    ('si', 6, 2),
+    ('ga', 6, 0, 's'),
+    ('qy', 5),
+    ('sc', 5),
+    ('s3', 6, 3, 0),
+    ('s3', 6, 3, 1),
+    ('s3', 6, 3, 2),
+    ('si', 6, 3),
+    ('s3', 7, 0, 0),
+    ('s3', 7, 0, 1),
+    ('s3', 7, 0, 2),
+    ('si', 7, 0),
+    ('ga', 6, 1, 'v'),
+    ('s3', 7, 1, 0),
+    ('s3', 7, 1, 1),
+    ('s3', 7, 1, 2),
+    ('si', 7, 1),
+    ('ga', 6, 2, 'v'),
+    ('ga', 6, 3, 'v'),
+    ('ga', 7, 0, 'v'),
+    ('ty', 5, 2),
+    ('ty', 5, 3),
+    ('cy', 5, 2, 's'),
+    ('cy', 5, 3, 'v'),
+    ('sy', 5, 2, 4),
+    ('ty', 6, 0),
+    ('ty', 6, 1),
+    ('cy', 6, 0, 'v'),
+    ('cy', 6, 1, 's'),
+    ('sy', 6, 0, 2),
+    ('ty', 6, 2),
+    ('ty', 6, 3),
+    ('cy', 6, 2, 's'),
+    ('cy', 6, 3, 's'),
+    ('sy', 6, 2, 4),
+    ('gy', 6, 2, 'v'),
+    ('s3', 7, 2, 0),
+    ('s3', 7, 2, 1),
+    ('s3', 7, 2, 2),
+    ('si', 7, 2),
+    ('ga', 7, 1, 'v'),
+    ('qy', 6),
+    ('sc', 6),
+    ('s3', 7, 3, 0),
+    ('s3', 7, 3, 1),
+    ('s3', 7, 3, 2),
+    ('si', 7, 3),
+    ('ga', 7, 2, 'v'),
+    ('ga', 7, 3, 'v'),
+    ('ty', 7, 0),
+    ('ty', 7, 1),
+    ('cy', 7, 0, 'v'),
+    ('sy', 7, 0, 1),
+    ('cy', 7, 1, 'v'),
+    ('sy', 7, 1, 2),
+    ('ty', 7, 2),
+    ('ty', 7, 3),
+    ('cy', 7, 2, 's'),
+    ('sy', 7, 2, 3),
+    ('cy', 7, 3, 's'),
+    ('sy', 7, 3, 4),
+    ('gy', 7, 0, 'v'),
+    ('gy', 7, 1, 'v'),
+    ('qy', 7),
+    ('sc', 7),
+    ('ss', 1),
+]
 
 
 def tile_gated_lowrank_experts_projection_k1_kernel(
@@ -60,8 +496,11 @@ def tile_gated_lowrank_experts_projection_k1_kernel(
 
         ident = kept("ident", [P, P], F32)
         make_identity(nc, ident[:])
-        ws_raw = kept("ws_raw", [P, DG, N], U8)
-        nc.gpsimd.memset(ws_raw[:].rearrange("p g n -> p (g n)").bitcast(I32), 0)
+        ws_raw = kept("ws_raw", [P, N], U8)
+        nc.vector.memset(ws_raw[:].bitcast(I32), 0)
+        ws_rows = kept("ws_rows", [P, N], U8)
+        ws = kept("ws", [P, DG, N], U8)
+        nc.gpsimd.memset(ws[:].rearrange("p g n -> p (g n)").bitcast(I32), 0)
         warm = kept("warm", [P, 2], F32)
         nc.vector.memset(warm[:, 0:1], 0.0)
         nc.scalar.activation(out=warm[:, 1:2], in_=warm[:, 0:1], func=ACT.Silu)
@@ -73,11 +512,11 @@ def tile_gated_lowrank_experts_projection_k1_kernel(
         def wide(shape, dtype):
             return ring("wide", WIDE, shape, dtype)
 
-        def load_x(pr):
-            x_raw[pr] = wide([P, 2, D], BF16)
-            for i in range(2):
-                r0 = pr * PAIR + i * P
-                nc.sync.dma_start(out=x_raw[pr][:, i, :], in_=x[r0 : r0 + P, :])
+        def load_x(pr, i):
+            if pr not in x_raw:
+                x_raw[pr] = wide([P, 2, D], BF16)
+            r0 = pr * PAIR + i * P
+            nc.sync.dma_start(out=x_raw[pr][:, i, :], in_=x[r0 : r0 + P, :])
 
         def load_gates(pr):
             g_raw[pr] = ring("g_raw", 3, [P, 2, R], BF16)
@@ -99,10 +538,13 @@ def tile_gated_lowrank_experts_projection_k1_kernel(
             src = w_words[:, :, 2 * KP * n : 2 * KP * (n + 1)].rearrange("g p b -> p g b")
             nc.sync.dma_start(out=w_raw[n][:].bitcast(I32), in_=src.bitcast(I32))
 
+        def load_raw_scales():
+            nc.scalar.dma_start(out=ws_raw[: DG * 16, :].bitcast(I32), in_=w_scales.rearrange("g q n -> q g n").bitcast(I32))
+
         def load_w_scales():
             for q in range(4):
-                src = w_scales[:, 4 * q : 4 * q + 4, :].rearrange("g r n -> r g n")
-                nc.sync.dma_start(out=ws_raw[32 * q : 32 * q + 4, :, :].bitcast(I32), in_=src.bitcast(I32))
+                src = ws_rows[4 * DG * q : 4 * DG * (q + 1), :]
+                nc.sync.dma_start(out=ws[32 * q : 32 * q + 4, :, :].bitcast(I32), in_=src.bitcast(I32))
 
         def load_vectors():
             nc.sync.dma_start(out=bias_sb[:], in_=bias.rearrange("(g p t) -> p g t", p=P, t=PACK))
@@ -114,14 +556,20 @@ def tile_gated_lowrank_experts_projection_k1_kernel(
         dq, ds, uq, us, grouped = {}, {}, {}, {}, {}
         hb, hq, hs = {}, {}, {}
         x1q, x1s = {}, {}
-        wq, ws = {}, {}
+        wq = {}
 
-        def turn(raws, g, dst):
-            b, bank = take_bank()
+        held = {}
+
+        def turn(key, raw, g):
+            held[key] = take_bank()
+            bank = held[key][1]
             for i in range(2):
-                words = raws[i].bitcast(F32)
+                words = raw[:, i, :].bitcast(F32)
                 for u in range(2):
                     nc.tensor.transpose(bank[:, 2 * i + u, :], words[:, 256 * g + u : 256 * (g + 1) : 2], ident[:])
+
+        def gather(key, dst):
+            b, bank = held[key]
             nc.scalar.copy(
                 out=dst.bitcast(F32).rearrange("p (i r u) -> p i r u", i=2, u=2),
                 in_=bank[:].rearrange("p (i u) r -> p i r u", u=2),
@@ -129,30 +577,42 @@ def tile_gated_lowrank_experts_projection_k1_kernel(
             free_banks.append(b)
 
         def turn_x(pr, g):
+            turn(("x", pr, g), x_raw[pr], g)
+
+        def gather_x(pr, g):
             h = pr // 2
             if (h, g) not in xt:
                 xt[h, g] = kept("xt%d_%d" % (h, g), [P, 2, PAIR * PACK], BF16)
-            turn([x_raw[pr][:, 0, :], x_raw[pr][:, 1, :]], g, xt[h, g][:, pr % 2, :])
+            gather(("x", pr, g), xt[h, g][:, pr % 2, :])
 
         def turn_gates(pr):
+            turn(("g", pr), g_raw[pr], 0)
+
+        def gather_gates(pr):
             gt[pr] = ring("gt", 4, [P, PAIR * PACK], BF16)
-            turn([g_raw[pr][:, 0, :], g_raw[pr][:, 1, :]], 0, gt[pr][:])
+            gather(("g", pr), gt[pr][:])
 
         def quantize_x(pr, g):
             xq[pr, g] = ring("xq", 9, [P, PAIR], U32)
             xs[pr, g] = ring("xs", 9, [P, PAIR], U8)
             quantize(xq[pr, g][:], xs[pr, g][:], xt[pr // 2, g][:, pr % 2, :])
 
-        def group_factor(key, raw, engine):
-            grouped[key] = ring("grouped", 3, [P, KP * PACK], BF16)
-            dst = grouped[key][:].rearrange("p (t m j) -> p t m j", t=PACK, j=PACK)
-            src = raw[:].rearrange("p j (m t) -> p t m j", t=PACK)
+        def group_factor(name, g, part, engine):
+            key = (name, g)
+            raw = down_raw[g] if name == "down" else up_raw[g]
+            if key not in grouped:
+                grouped[key] = ring("grouped", 3, [P, KP * PACK], BF16)
+            span = slice(0, 64) if part == 2 else slice(32 * part, 32 * (part + 1))
+            dst = grouped[key][:].rearrange("p (t m i j) -> p m t i j", t=PACK, i=2, j=PACK)[:, span]
+            src = raw[:].rearrange("p j (m i t) -> p m t i j", i=2, t=PACK)[:, span]
             if engine == "v":
                 nc.vector.tensor_copy(out=dst, in_=src)
             else:
                 nc.scalar.copy(out=dst, in_=src)
 
-        def quantize_factor(key, codes, scales):
+        def quantize_factor(name, g):
+            key = (name, g)
+            codes, scales = (dq, ds) if name == "down" else (uq, us)
             codes[key[1]] = kept("%s_q%d" % key, [P, KP], U32)
             scales[key[1]] = kept("%s_s%d" % key, [P, KP], U8)
             quantize(codes[key[1]][:], scales[key[1]][:], grouped[key][:])
@@ -164,17 +624,17 @@ def tile_gated_lowrank_experts_projection_k1_kernel(
                 in_=w_raw[n][:, g, :].rearrange("p (m t b) -> p t m b", t=PACK, b=2),
             )
 
-        def order_w_scales(n):
-            ws[n] = kept("ws%d" % n, [P, DG, KP], U8)
+        def order_w_scales():
             nc.vector.tensor_copy(
-                out=ws[n][:].rearrange("p g (t m) -> p g t m", t=PACK),
-                in_=ws_raw[:, :, n * KP : (n + 1) * KP].rearrange("p g (m t) -> p g t m", t=PACK),
+                out=ws_rows[:].rearrange("p (n t m) -> p n t m", n=NG, t=PACK),
+                in_=ws_raw[:].rearrange("p (n m t) -> p n t m", n=NG, t=PACK),
             )
 
         def stage1(i):
             pr = i // 2
             tok = slice((i % 2) * P, (i % 2 + 1) * P)
-            b, bank = take_bank()
+            held["z", i] = take_bank()
+            bank = held["z", i][1]
             for t in range(PACK):
                 col = slice(t * P, (t + 1) * P)
                 for g in range(DG):
@@ -183,6 +643,10 @@ def tile_gated_lowrank_experts_projection_k1_kernel(
                         rhs=xq[pr, g][:, tok].bitcast(FP8X4), rhs_scale=xs[pr, g][:, tok],
                         start=(g == 0), stop=(g == DG - 1),
                     )
+
+        def gate(i):
+            pr = i // 2
+            b, bank = held["z", i]
             if pr not in hb:
                 hb[pr] = ring("hb", 2, [P, PAIR * PACK], BF16)
             span = slice((i % 2) * KP, (i % 2 + 1) * KP)
@@ -202,13 +666,18 @@ def tile_gated_lowrank_experts_projection_k1_kernel(
         def stage2(i, g):
             pr = i // 2
             tok = slice((i % 2) * P, (i % 2 + 1) * P)
-            b, bank = take_bank()
+            held["u", i, g] = take_bank()
+            bank = held["u", i, g][1]
             for t in range(PACK):
                 col = slice(t * P, (t + 1) * P)
                 nc.tensor.matmul_mx(
                     out=bank[:, t, :], lhsT=uq[g][:, col].bitcast(FP8X4), lhsT_scale=us[g][:, col],
                     rhs=hq[pr][:, tok].bitcast(FP8X4), rhs_scale=hs[pr][:, tok], start=True, stop=True,
                 )
+
+        def correct(i, g):
+            pr = i // 2
+            b, bank = held["u", i, g]
             span = slice((i % 2) * KP, (i % 2 + 1) * KP)
             x_part = xt[i // 4, g][:, pr % 2, span].rearrange("p (r t) -> p r t", t=PACK)
             nc.vector.tensor_tensor(out=x_part, in0=bank[:].rearrange("p t r -> p r t"), in1=x_part, op=ALU.add)
@@ -220,7 +689,7 @@ def tile_gated_lowrank_experts_projection_k1_kernel(
             quantize(x1q[h, g][:], x1s[h, g][:], xt[h, g][:].rearrange("p i c -> p (i c)"))
 
         yt, acc, yb = {}, {}, {}
-        y_scales = [kept("y_scales%d" % h, [P, NG, HALF], U8) for h in range(2)]
+        y_scales = [kept("y_scales%d" % h, [P, HALF], U8) for h in range(2)]
 
         def stage3_pass(k, t, g):
             h, n = divmod(k, NG)
@@ -229,14 +698,14 @@ def tile_gated_lowrank_experts_projection_k1_kernel(
             nc.tensor.matmul_mx(
                 out=acc[k, t][1][:].rearrange("p a b -> p (a b)"),
                 lhsT=wq[n, g][:, 2 * P * t : 2 * P * (t + 1)].bitcast(FP4X4),
-                lhsT_scale=ws[n][:, g, P * t : P * (t + 1)],
+                lhsT_scale=ws[:, g, KP * n + P * t : KP * n + P * (t + 1)],
                 rhs=x1q[h, g][:].bitcast(FP8X4), rhs_scale=x1s[h, g][:],
                 start=(g == 0), stop=(g == DG - 1),
             )
 
         def silu(k, t):
             n = k % NG
-            if t == 0:
+            if k not in yt:
                 yt[k] = wide([P, PACK, HALF], F32)
             b, bank = acc[k, t]
             nc.scalar.activation(
@@ -245,187 +714,80 @@ def tile_gated_lowrank_experts_projection_k1_kernel(
             )
             free_banks.append(b)
 
-        def apply_gain(k, t):
+        def apply_gain(k, t, on):
             factor = gain_f32[:, k % NG, t : t + 1]
-            if GAIN_ON[k] == "v":
+            if on == "v":
                 nc.vector.tensor_scalar(
                     out=yt[k][:, t, :], in0=yt[k][:, t, :], scalar1=factor, scalar2=None, op0=ALU.mult
                 )
             else:
                 nc.scalar.activation(out=yt[k][:, t, :], in_=yt[k][:, t, :], func=ACT.Copy, scale=factor)
 
-        def turn_y(k, on):
-            h, n = divmod(k, NG)
-            banks = []
-            for i in range(4):
-                b, bank = take_bank()
-                banks.append((b, bank))
-                for t in range(PACK):
-                    nc.tensor.transpose(bank[:, t, :], yt[k][:, t, i * P : (i + 1) * P], ident[:])
-            for i in range(4):
-                b, bank = banks[i]
-                rows = ring("y_rows", 8, [P, KP], F32)
-                dst = rows[:].rearrange("r (p t) -> r p t", t=PACK)
-                src = bank[:].rearrange("r t p -> r p t")
-                if on[i] == "v":
-                    nc.vector.tensor_copy(out=dst, in_=src)
-                else:
-                    nc.scalar.copy(out=dst, in_=src)
-                free_banks.append(b)
-                r0 = h * HALF + i * P
-                nc.sync.dma_start(out=out_0[r0 : r0 + P, n * KP : (n + 1) * KP], in_=rows[:])
+        def turn_y(k, i):
+            held["y", k, i] = take_bank()
+            bank = held["y", k, i][1]
+            for t in range(PACK):
+                nc.tensor.transpose(bank[:, t, :], yt[k][:, t, i * P : (i + 1) * P], ident[:])
 
-        def group_y(k):
-            yb[k] = ring("yb", 2, [P, HALF * PACK], BF16)
-            nc.vector.tensor_copy(
-                out=yb[k][:].rearrange("p (r t) -> p r t", t=PACK), in_=yt[k][:].rearrange("p t r -> p r t")
-            )
+        y_rows = {}
+
+        def gather_y(k, i, on):
+            b, bank = held["y", k, i]
+            if (k, i // 2) not in y_rows:
+                y_rows[k, i // 2] = ring("y_rows", 4, [P, 2, KP], F32)
+            dst = y_rows[k, i // 2][:, i % 2, :].rearrange("r (p t) -> r p t", t=PACK)
+            src = bank[:].rearrange("r t p -> r p t")
+            if on == "v":
+                nc.vector.tensor_copy(out=dst, in_=src)
+            else:
+                nc.scalar.copy(out=dst, in_=src)
+            free_banks.append(b)
+
+        def store_y(k, i0, i1):
+            h, n = divmod(k, NG)
+            rows = out_0[h * HALF + i0 * P : h * HALF + i1 * P, n * KP : (n + 1) * KP]
+            src = y_rows[k, i0 // 2][:, i0 % 2 : i0 % 2 + i1 - i0, :]
+            nc.sync.dma_start(out=rows.rearrange("(i p) n -> p i n", p=P), in_=src)
+
+        y_codes = {}
+
+        def group_y(k, part, engine):
+            if k not in yb:
+                yb[k] = ring("yb", 2, [P, HALF * PACK], BF16)
+            span = slice(0, 128) if part == 2 else slice(64 * part, 64 * (part + 1))
+            dst = yb[k][:].rearrange("p (c i t) -> p c t i", i=4, t=PACK)[:, span]
+            src = yt[k][:].rearrange("p t (c i) -> p c t i", i=4)[:, span]
+            if engine == "v":
+                nc.vector.tensor_copy(out=dst, in_=src)
+            else:
+                nc.scalar.copy(out=dst, in_=src)
 
         def quantize_y(k):
             h, n = divmod(k, NG)
-            codes = ring("y_codes", 3, [P, HALF], U32)
-            quantize(codes[:], y_scales[h][:, n, :], yb[k][:])
+            y_codes[k] = ring("y_codes", 3, [P, HALF], U32)
+            quantize(y_codes[k][:], y_scales[h][4 * n :, :], yb[k][:])
+
+        def store_codes(k):
+            h, n = divmod(k, NG)
             dst = out_1[n, :, h * HALF : (h + 1) * HALF, :].rearrange("p m t -> p (m t)")
-            nc.sync.dma_start(out=dst.bitcast(I32), in_=codes[:].bitcast(I32))
+            nc.sync.dma_start(out=dst.bitcast(I32), in_=y_codes[k][:].bitcast(I32))
 
-        def store_y_scales(h, n0, n1):
-            tok = slice(h * HALF, (h + 1) * HALF)
+        def store_y_scales(h):
             for q in range(4):
-                dst = out_2[n0:n1, 4 * q : 4 * q + 4, tok].rearrange("g r m -> r g m")
-                nc.sync.dma_start(out=dst.bitcast(I32), in_=y_scales[h][32 * q : 32 * q + 4, n0:n1, :].bitcast(I32))
+                dst = out_2[:, 4 * q : 4 * q + 4, h * HALF : (h + 1) * HALF]
+                nc.sync.dma_start(out=dst.bitcast(I32), in_=y_scales[h][32 * q : 32 * q + 16, :].bitcast(I32))
 
-        load_down(0)
-        load_x(0)
-        load_down(1)
-        load_down(2)
-        load_gates(0)
-        load_up(0)
-        load_x(1)
-        load_gates(1)
-        load_up(1)
-        load_up(2)
-        load_w_scales()
-        load_w(0)
-        load_vectors()
 
-        group_factor(("down", 0), down_raw[0], DOWN_ON[0])
-        load_x(2)
-        load_gates(2)
-        for g in range(DG):
-            turn_x(0, g)
-        turn_gates(0)
-        quantize_factor(("down", 0), dq, ds)
-        group_factor(("down", 1), down_raw[1], DOWN_ON[1])
-        quantize_x(0, 0)
-        group_factor(("down", 2), down_raw[2], DOWN_ON[2])
-        load_w(1)
-        load_x(3)
-        load_gates(3)
-        load_w(2)
-        load_w(3)
-        quantize_factor(("down", 1), dq, ds)
-        quantize_x(0, 1)
-        quantize_x(0, 2)
-        quantize_factor(("down", 2), dq, ds)
-        group_factor(("up", 0), up_raw[0], UP_ON[0])
-        stage1(0)
-        stage1(1)
-        for g in range(DG):
-            turn_x(1, g)
-        turn_gates(1)
-        quantize_factor(("up", 0), uq, us)
-        quantize_h(0)
-        for g in range(DG):
-            quantize_x(1, g)
-        group_factor(("up", 1), up_raw[1], UP_ON[1])
-        stage2(0, 0)
-        stage2(1, 0)
-        stage1(2)
-        stage1(3)
-        group_factor(("up", 2), up_raw[2], UP_ON[2])
-        nc.scalar.copy(out=gain_f32[:], in_=gain_sb[:])
-        quantize_factor(("up", 1), uq, us)
-        quantize_h(1)
-        stage2(0, 1)
-        stage2(1, 1)
-        stage2(2, 0)
-        stage2(3, 0)
-        for g in range(DG):
-            turn_x(2, g)
-        turn_gates(2)
-        order_w_scales(0)
-        quantize_x1(0, 0)
-        stage2(2, 1)
-        stage2(3, 1)
-        quantize_factor(("up", 2), uq, us)
-        order_w_codes(0, 0)
-        quantize_x1(0, 1)
-        for g in range(DG):
-            turn_x(3, g)
-        turn_gates(3)
-        stage2(0, 2)
-        order_w_codes(0, 1)
-        for i in range(1, 4):
-            stage2(i, 2)
-        for g in range(2):
-            for t in range(PACK):
-                stage3_pass(0, t, g)
-        order_w_codes(0, 2)
-        quantize_x1(0, 2)
+        def widen_gain():
+            nc.scalar.copy(out=gain_f32[:], in_=gain_sb[:])
 
-        extra = {}
-
-        def later(s, *job):
-            extra.setdefault(s, []).append(job)
-
-        for g in range(DG):
-            later(0, quantize_x, 2, g)
-        later(0, stage1, 4)
-        later(1, order_w_scales, 1)
-        later(1, stage1, 5)
-        for g in range(DG):
-            later(1 + g, order_w_codes, 1, g)
-        for n in range(2, NG):
-            later(4 * n - 4, order_w_scales, n)
-            for g in range(DG):
-                later(4 * n - 4 + g, order_w_codes, n, g)
-        for g in range(DG):
-            later(3, quantize_x, 3, g)
-        later(4, stage1, 6)
-        later(2, quantize_h, 2)
-        later(5, stage1, 7)
-        later(6, stage2, 4, 0)
-        later(6, quantize_h, 3)
-        slots = {(5, 0): 7, (6, 0): 7, (7, 0): 8, (4, 1): 9, (5, 1): 10, (6, 1): 11, (7, 1): 11,
-                 (4, 2): 12, (5, 2): 12, (6, 2): 13, (7, 2): 13}
-        for (i, g), s in slots.items():
-            later(s, stage2, i, g)
-            if i == 7:
-                later(s + 1, quantize_x1, 1, g)
-        units = 2 * NG
-        planes_at = PLANES_AT
-        for k, s in planes_at.items():
-            later(s, group_y, k)
-            later(s + 1, quantize_y, k)
-        later(planes_at[3] + 2, store_y_scales, 0, 0, NG)
-        later(planes_at[6] + 2, store_y_scales, 1, 0, NG - 1)
-
-        for k in range(units):
-            for t in range(PACK):
-                for g in range(DG):
-                    if k > 0 or g == DG - 1:
-                        stage3_pass(k, t, g)
-                silu(k, t)
-                if t > 0:
-                    apply_gain(k, t - 1)
-                elif k > 0:
-                    apply_gain(k - 1, PACK - 1)
-                for job in extra.get(PACK * k + t, []):
-                    job[0](*job[1:])
-                if k > 0 and t == TURN_AT:
-                    turn_y(k - 1, COPY_ON[k - 1])
-        apply_gain(units - 1, PACK - 1)
-        group_y(units - 1)
-        quantize_y(units - 1)
-        turn_y(units - 1, COPY_ON[units - 1])
-        store_y_scales(1, NG - 1, NG)
+        jobs = {
+            "lx": load_x, "lg": load_gates, "ld": load_down, "lu": load_up, "lw": load_w, "ls": load_w_scales,
+            "lv": load_vectors, "lr": load_raw_scales, "wg": widen_gain, "tx": turn_x, "cx": gather_x, "tg": turn_gates, "cg": gather_gates,
+            "qx": quantize_x, "gf": group_factor, "qf": quantize_factor, "wc": order_w_codes, "ws": order_w_scales,
+            "s1": stage1, "h": gate, "qh": quantize_h, "s2": stage2, "x1": correct, "q1": quantize_x1,
+            "s3": stage3_pass, "si": silu, "ga": apply_gain, "ty": turn_y, "cy": gather_y, "sy": store_y,
+            "gy": group_y, "qy": quantize_y, "sc": store_codes, "ss": store_y_scales,
+        }
+        for job in ORDER:
+            jobs[job[0]](*job[1:])

from contextlib import ExitStack

import concourse.mybir as mybir
from concourse.masks import make_identity

M, D, R, N = 1024, 1536, 512, 2048
FLOPS = 2 * M * (D * R + R * D + D * N)

F32 = mybir.dt.float32
BF16 = mybir.dt.bfloat16
I32 = mybir.dt.int32
U32 = mybir.dt.uint32
U8 = mybir.dt.uint8
FP8X4 = mybir.dt.float8_e4m3fn_x4
FP4X4 = mybir.dt.float4_e2m1fn_x4
ALU = mybir.AluOpType
ACT = mybir.ActivationFunctionType

P = 128
PACK = 4
KP = P * PACK
DG = D // KP
NG = N // KP
PAIR = 2 * P
HALF = 4 * P
WIDE = 8
ORDER = [
    ('ld', 0),
    ('gf', 'down', 0, 0, 'v'),
    ('gf', 'down', 0, 1, 's'),
    ('ld', 1),
    ('lx', 0, 0),
    ('lx', 0, 1),
    ('ld', 2),
    ('gf', 'down', 1, 0, 'v'),
    ('lx', 1, 0),
    ('lx', 1, 1),
    ('lr',),
    ('tx', 0, 0),
    ('cx', 0, 0),
    ('gf', 'down', 1, 1, 'v'),
    ('tx', 0, 1),
    ('cx', 0, 1),
    ('lg', 0),
    ('lw', 0),
    ('tx', 0, 2),
    ('cx', 0, 2),
    ('qf', 'down', 0),
    ('tx', 1, 0),
    ('cx', 1, 0),
    ('tx', 1, 1),
    ('cx', 1, 1),
    ('lu', 0),
    ('qf', 'down', 1),
    ('tx', 1, 2),
    ('cx', 1, 2),
    ('gf', 'down', 2, 0, 'v'),
    ('tg', 0),
    ('cg', 0),
    ('gf', 'down', 2, 1, 'v'),
    ('lg', 1),
    ('qx', 0, 0),
    ('qf', 'down', 2),
    ('qx', 0, 1),
    ('qx', 0, 2),
    ('ws',),
    ('gf', 'up', 0, 2, 's'),
    ('qx', 1, 0),
    ('wc', 0, 0),
    ('qx', 1, 1),
    ('wc', 0, 1),
    ('qx', 1, 2),
    ('s1', 0),
    ('h', 0),
    ('lx', 2, 0),
    ('lu', 1),
    ('s1', 1),
    ('h', 1),
    ('lg', 2),
    ('wc', 0, 2),
    ('tg', 1),
    ('cg', 1),
    ('gf', 'up', 1, 2, 's'),
    ('qh', 0),
    ('lx', 2, 1),
    ('qf', 'up', 0),
    ('s1', 2),
    ('h', 2),
    ('s1', 3),
    ('h', 3),
    ('s2', 0, 0),
    ('x1', 0, 0),
    ('lu', 2),
    ('tg', 2),
    ('cg', 2),
    ('qh', 1),
    ('s2', 1, 0),
    ('x1', 1, 0),
    ('gf', 'up', 2, 2, 's'),
    ('qf', 'up', 1),
    ('tx', 2, 0),
    ('cx', 2, 0),
    ('s2', 2, 0),
    ('x1', 2, 0),
    ('s2', 3, 0),
    ('x1', 3, 0),
    ('s2', 0, 1),
    ('x1', 0, 1),
    ('lg', 3),
    ('s2', 1, 1),
    ('x1', 1, 1),
    ('tx', 2, 1),
    ('cx', 2, 1),
    ('tx', 2, 2),
    ('cx', 2, 2),
    ('qf', 'up', 2),
    ('q1', 0, 0),
    ('tg', 3),
    ('cg', 3),
    ('ls',),
    ('s2', 2, 1),
    ('x1', 2, 1),
    ('s2', 3, 1),
    ('x1', 3, 1),
    ('lx', 3, 0),
    ('s2', 0, 2),
    ('x1', 0, 2),
    ('s2', 1, 2),
    ('x1', 1, 2),
    ('s2', 2, 2),
    ('x1', 2, 2),
    ('q1', 0, 1),
    ('s3', 0, 0, 0),
    ('s3', 0, 1, 0),
    ('s2', 3, 2),
    ('x1', 3, 2),
    ('q1', 0, 2),
    ('qx', 2, 0),
    ('s3', 0, 2, 0),
    ('lx', 3, 1),
    ('s3', 0, 3, 0),
    ('tx', 3, 0),
    ('cx', 3, 0),
    ('tx', 3, 1),
    ('cx', 3, 1),
    ('qx', 2, 1),
    ('tx', 3, 2),
    ('cx', 3, 2),
    ('lw', 1),
    ('s3', 0, 0, 1),
    ('s3', 0, 1, 1),
    ('lv',),
    ('lw', 2),
    ('qx', 2, 2),
    ('s3', 0, 2, 1),
    ('s3', 0, 3, 1),
    ('qx', 3, 0),
    ('wg',),
    ('s3', 0, 0, 2),
    ('si', 0, 0),
    ('wc', 1, 0),
    ('wc', 1, 1),
    ('wc', 1, 2),
    ('s3', 0, 1, 2),
    ('si', 0, 1),
    ('qx', 3, 1),
    ('qx', 3, 2),
    ('s3', 0, 2, 2),
    ('si', 0, 2),
    ('ga', 0, 0, 's'),
    ('ga', 0, 1, 's'),
    ('s1', 4),
    ('h', 4),
    ('lw', 3),
    ('s3', 0, 3, 2),
    ('si', 0, 3),
    ('s1', 5),
    ('h', 5),
    ('s3', 1, 0, 0),
    ('s3', 1, 0, 1),
    ('s3', 1, 0, 2),
    ('si', 1, 0),
    ('ga', 0, 2, 's'),
    ('ga', 0, 3, 's'),
    ('wc', 2, 0),
    ('wc', 2, 1),
    ('qh', 2),
    ('s3', 1, 1, 0),
    ('s3', 1, 1, 1),
    ('s3', 1, 1, 2),
    ('si', 1, 1),
    ('wc', 2, 2),
    ('s3', 1, 2, 0),
    ('s3', 1, 2, 1),
    ('s3', 1, 2, 2),
    ('si', 1, 2),
    ('ga', 1, 0, 'v'),
    ('ga', 1, 1, 'v'),
    ('ga', 1, 2, 'v'),
    ('gy', 0, 2, 's'),
    ('s1', 6),
    ('h', 6),
    ('s1', 7),
    ('h', 7),
    ('s2', 4, 0),
    ('x1', 4, 0),
    ('qh', 3),
    ('s3', 1, 3, 0),
    ('s3', 1, 3, 1),
    ('s3', 1, 3, 2),
    ('si', 1, 3),
    ('s3', 2, 0, 0),
    ('s3', 2, 0, 1),
    ('s3', 2, 0, 2),
    ('si', 2, 0),
    ('ga', 1, 3, 's'),
    ('qy', 0),
    ('sc', 0),
    ('s2', 5, 0),
    ('x1', 5, 0),
    ('s2', 4, 1),
    ('x1', 4, 1),
    ('s3', 2, 1, 0),
    ('s3', 2, 1, 1),
    ('s3', 2, 1, 2),
    ('si', 2, 1),
    ('ga', 2, 0, 's'),
    ('ga', 2, 1, 's'),
    ('s2', 6, 0),
    ('x1', 6, 0),
    ('s2', 7, 0),
    ('x1', 7, 0),
    ('s2', 5, 1),
    ('x1', 5, 1),
    ('s2', 6, 1),
    ('x1', 6, 1),
    ('s3', 2, 2, 0),
    ('s3', 2, 2, 1),
    ('s3', 2, 2, 2),
    ('si', 2, 2),
    ('ty', 0, 0),
    ('ty', 0, 1),
    ('cy', 0, 0, 's'),
    ('cy', 0, 1, 'v'),
    ('sy', 0, 0, 2),
    ('ty', 0, 2),
    ('ty', 0, 3),
    ('cy', 0, 2, 's'),
    ('cy', 0, 3, 's'),
    ('sy', 0, 2, 4),
    ('ty', 1, 0),
    ('ty', 1, 1),
    ('cy', 1, 0, 's'),
    ('cy', 1, 1, 's'),
    ('sy', 1, 0, 2),
    ('ty', 1, 2),
    ('ty', 1, 3),
    ('cy', 1, 2, 's'),
    ('cy', 1, 3, 's'),
    ('sy', 1, 2, 4),
    ('wc', 3, 0),
    ('wc', 3, 1),
    ('wc', 3, 2),
    ('s2', 7, 1),
    ('x1', 7, 1),
    ('s2', 4, 2),
    ('x1', 4, 2),
    ('s2', 5, 2),
    ('x1', 5, 2),
    ('s2', 6, 2),
    ('x1', 6, 2),
    ('s2', 7, 2),
    ('x1', 7, 2),
    ('s3', 2, 3, 0),
    ('s3', 2, 3, 1),
    ('s3', 2, 3, 2),
    ('si', 2, 3),
    ('q1', 1, 0),
    ('s3', 3, 0, 0),
    ('s3', 3, 0, 1),
    ('s3', 3, 0, 2),
    ('si', 3, 0),
    ('ga', 2, 2, 'v'),
    ('ga', 2, 3, 's'),
    ('ga', 3, 0, 's'),
    ('q1', 1, 1),
    ('q1', 1, 2),
    ('s3', 3, 1, 0),
    ('s3', 3, 1, 1),
    ('s3', 3, 1, 2),
    ('si', 3, 1),
    ('gy', 1, 2, 'v'),
    ('s3', 3, 2, 0),
    ('s3', 3, 2, 1),
    ('s3', 3, 2, 2),
    ('si', 3, 2),
    ('s3', 3, 3, 0),
    ('s3', 3, 3, 1),
    ('s3', 3, 3, 2),
    ('si', 3, 3),
    ('ga', 3, 1, 's'),
    ('s3', 4, 0, 0),
    ('s3', 4, 0, 1),
    ('s3', 4, 0, 2),
    ('si', 4, 0),
    ('ga', 3, 2, 'v'),
    ('ga', 3, 3, 'v'),
    ('qy', 1),
    ('sc', 1),
    ('s3', 4, 1, 0),
    ('s3', 4, 1, 1),
    ('s3', 4, 1, 2),
    ('si', 4, 1),
    ('ga', 4, 0, 's'),
    ('ty', 2, 0),
    ('ty', 2, 1),
    ('cy', 2, 0, 's'),
    ('cy', 2, 1, 'v'),
    ('sy', 2, 0, 2),
    ('ty', 2, 2),
    ('ty', 2, 3),
    ('cy', 2, 2, 'v'),
    ('cy', 2, 3, 's'),
    ('sy', 2, 2, 4),
    ('ty', 3, 0),
    ('ty', 3, 1),
    ('cy', 3, 0, 'v'),
    ('cy', 3, 1, 's'),
    ('sy', 3, 0, 2),
    ('gy', 2, 2, 'v'),
    ('gy', 3, 2, 'v'),
    ('qy', 2),
    ('sc', 2),
    ('s3', 4, 2, 0),
    ('s3', 4, 2, 1),
    ('s3', 4, 2, 2),
    ('si', 4, 2),
    ('s3', 4, 3, 0),
    ('s3', 4, 3, 1),
    ('s3', 4, 3, 2),
    ('si', 4, 3),
    ('ga', 4, 1, 's'),
    ('s3', 5, 0, 0),
    ('s3', 5, 0, 1),
    ('s3', 5, 0, 2),
    ('si', 5, 0),
    ('ga', 4, 2, 'v'),
    ('ga', 4, 3, 'v'),
    ('ga', 5, 0, 'v'),
    ('s3', 5, 1, 0),
    ('s3', 5, 1, 1),
    ('s3', 5, 1, 2),
    ('si', 5, 1),
    ('qy', 3),
    ('sc', 3),
    ('s3', 5, 2, 0),
    ('s3', 5, 2, 1),
    ('s3', 5, 2, 2),
    ('si', 5, 2),
    ('ga', 5, 1, 'v'),
    ('ss', 0),
    ('s3', 5, 3, 0),
    ('s3', 5, 3, 1),
    ('s3', 5, 3, 2),
    ('si', 5, 3),
    ('ga', 5, 2, 'v'),
    ('ga', 5, 3, 'v'),
    ('ty', 3, 2),
    ('ty', 3, 3),
    ('cy', 3, 2, 'v'),
    ('cy', 3, 3, 's'),
    ('sy', 3, 2, 4),
    ('ty', 4, 0),
    ('ty', 4, 1),
    ('cy', 4, 0, 's'),
    ('cy', 4, 1, 's'),
    ('sy', 4, 0, 2),
    ('ty', 4, 2),
    ('ty', 4, 3),
    ('cy', 4, 2, 'v'),
    ('cy', 4, 3, 'v'),
    ('sy', 4, 2, 4),
    ('ty', 5, 0),
    ('ty', 5, 1),
    ('cy', 5, 0, 's'),
    ('cy', 5, 1, 's'),
    ('sy', 5, 0, 2),
    ('gy', 4, 2, 'v'),
    ('s3', 6, 0, 0),
    ('s3', 6, 0, 1),
    ('s3', 6, 0, 2),
    ('si', 6, 0),
    ('gy', 5, 2, 'v'),
    ('qy', 4),
    ('sc', 4),
    ('s3', 6, 1, 0),
    ('s3', 6, 1, 1),
    ('s3', 6, 1, 2),
    ('si', 6, 1),
    ('s3', 6, 2, 0),
    ('s3', 6, 2, 1),
    ('s3', 6, 2, 2),
    ('si', 6, 2),
    ('ga', 6, 0, 's'),
    ('qy', 5),
    ('sc', 5),
    ('s3', 6, 3, 0),
    ('s3', 6, 3, 1),
    ('s3', 6, 3, 2),
    ('si', 6, 3),
    ('s3', 7, 0, 0),
    ('s3', 7, 0, 1),
    ('s3', 7, 0, 2),
    ('si', 7, 0),
    ('ga', 6, 1, 'v'),
    ('s3', 7, 1, 0),
    ('s3', 7, 1, 1),
    ('s3', 7, 1, 2),
    ('si', 7, 1),
    ('ga', 6, 2, 'v'),
    ('ga', 6, 3, 'v'),
    ('ga', 7, 0, 'v'),
    ('ty', 5, 2),
    ('ty', 5, 3),
    ('cy', 5, 2, 's'),
    ('cy', 5, 3, 'v'),
    ('sy', 5, 2, 4),
    ('ty', 6, 0),
    ('ty', 6, 1),
    ('cy', 6, 0, 'v'),
    ('cy', 6, 1, 's'),
    ('sy', 6, 0, 2),
    ('ty', 6, 2),
    ('ty', 6, 3),
    ('cy', 6, 2, 's'),
    ('cy', 6, 3, 's'),
    ('sy', 6, 2, 4),
    ('gy', 6, 2, 'v'),
    ('s3', 7, 2, 0),
    ('s3', 7, 2, 1),
    ('s3', 7, 2, 2),
    ('si', 7, 2),
    ('ga', 7, 1, 'v'),
    ('qy', 6),
    ('sc', 6),
    ('s3', 7, 3, 0),
    ('s3', 7, 3, 1),
    ('s3', 7, 3, 2),
    ('si', 7, 3),
    ('ga', 7, 2, 'v'),
    ('ga', 7, 3, 'v'),
    ('ty', 7, 0),
    ('ty', 7, 1),
    ('cy', 7, 0, 'v'),
    ('sy', 7, 0, 1),
    ('cy', 7, 1, 'v'),
    ('sy', 7, 1, 2),
    ('ty', 7, 2),
    ('ty', 7, 3),
    ('cy', 7, 2, 's'),
    ('sy', 7, 2, 3),
    ('cy', 7, 3, 's'),
    ('sy', 7, 3, 4),
    ('gy', 7, 0, 'v'),
    ('gy', 7, 1, 'v'),
    ('qy', 7),
    ('sc', 7),
    ('ss', 1),
]


def tile_gated_lowrank_experts_projection_k1_kernel(
    tc, x, down, gates, up, w_words, w_scales, bias, gain, out_0, out_1, out_2
):
    nc = tc.nc
    with ExitStack() as ctx:
        keep = ctx.enter_context(tc.tile_pool(name="keep", bufs=1))
        psum = ctx.enter_context(tc.psum_pool(name="psum", bufs=1))
        ctx.enter_context(tc.manual_schedule())

        def kept(name, shape, dtype):
            return keep.tile(shape, dtype, name=name, align_bytes=64)

        def ring(tag, bufs, shape, dtype):
            return keep.tile(shape, dtype, name=tag, tag=tag, bufs=bufs, align_bytes=64)

        free_banks = list(range(8))

        def take_bank():
            b = free_banks.pop(0)
            bank = psum.tile([P, PACK, P], F32, name="bank%d" % b, tag="bank%d" % b)
            return b, bank

        def quantize(codes, scales, src):
            nc.vector.quantize_mx(out=codes.bitcast(FP8X4), scales=scales, in_=src)

        ident = kept("ident", [P, P], F32)
        make_identity(nc, ident[:])
        ws_raw = kept("ws_raw", [P, N], U8)
        nc.vector.memset(ws_raw[:].bitcast(I32), 0)
        ws_rows = kept("ws_rows", [P, N], U8)
        ws = kept("ws", [P, DG, N], U8)
        nc.gpsimd.memset(ws[:].rearrange("p g n -> p (g n)").bitcast(I32), 0)
        warm = kept("warm", [P, 2], F32)
        nc.vector.memset(warm[:, 0:1], 0.0)
        nc.scalar.activation(out=warm[:, 1:2], in_=warm[:, 0:1], func=ACT.Silu)
        bias_sb = kept("bias_sb", [P, NG, PACK], BF16)
        gain_sb = kept("gain_sb", [P, NG, PACK], BF16)

        x_raw, g_raw, down_raw, up_raw, w_raw = {}, {}, {}, {}, {}

        def wide(shape, dtype):
            return ring("wide", WIDE, shape, dtype)

        def load_x(pr, i):
            if pr not in x_raw:
                x_raw[pr] = wide([P, 2, D], BF16)
            r0 = pr * PAIR + i * P
            nc.sync.dma_start(out=x_raw[pr][:, i, :], in_=x[r0 : r0 + P, :])

        def load_gates(pr):
            g_raw[pr] = ring("g_raw", 3, [P, 2, R], BF16)
            rows = gates[pr * PAIR : (pr + 1) * PAIR, :]
            nc.sync.dma_start(out=g_raw[pr][:], in_=rows.rearrange("(i p) r -> p i r", p=P))

        def load_down(g):
            down_raw[g] = wide([P, PACK, KP], BF16)
            rows = down[g * KP : (g + 1) * KP, :]
            nc.sync.dma_start(out=down_raw[g][:], in_=rows.rearrange("(p j) c -> p j c", j=PACK))

        def load_up(g):
            up_raw[g] = wide([P, PACK, KP], BF16)
            cols = up[:, g * KP : (g + 1) * KP]
            nc.sync.dma_start(out=up_raw[g][:], in_=cols.rearrange("(p j) c -> p j c", j=PACK))

        def load_w(n):
            w_raw[n] = ring("w_raw", 4, [P, DG, 2 * KP], U8)
            src = w_words[:, :, 2 * KP * n : 2 * KP * (n + 1)].rearrange("g p b -> p g b")
            nc.sync.dma_start(out=w_raw[n][:].bitcast(I32), in_=src.bitcast(I32))

        def load_raw_scales():
            nc.scalar.dma_start(out=ws_raw[: DG * 16, :].bitcast(I32), in_=w_scales.rearrange("g q n -> q g n").bitcast(I32))

        def load_w_scales():
            for q in range(4):
                src = ws_rows[4 * DG * q : 4 * DG * (q + 1), :]
                nc.sync.dma_start(out=ws[32 * q : 32 * q + 4, :, :].bitcast(I32), in_=src.bitcast(I32))

        def load_vectors():
            nc.sync.dma_start(out=bias_sb[:], in_=bias.rearrange("(g p t) -> p g t", p=P, t=PACK))
            nc.sync.dma_start(out=gain_sb[:], in_=gain.rearrange("(g p t) -> p g t", p=P, t=PACK))

        gain_f32 = kept("gain_f32", [P, NG, PACK], F32)

        xt, xq, xs, gt = {}, {}, {}, {}
        dq, ds, uq, us, grouped = {}, {}, {}, {}, {}
        hb, hq, hs = {}, {}, {}
        x1q, x1s = {}, {}
        wq = {}

        held = {}

        def turn(key, raw, g):
            held[key] = take_bank()
            bank = held[key][1]
            for i in range(2):
                words = raw[:, i, :].bitcast(F32)
                for u in range(2):
                    nc.tensor.transpose(bank[:, 2 * i + u, :], words[:, 256 * g + u : 256 * (g + 1) : 2], ident[:])

        def gather(key, dst):
            b, bank = held[key]
            nc.scalar.copy(
                out=dst.bitcast(F32).rearrange("p (i r u) -> p i r u", i=2, u=2),
                in_=bank[:].rearrange("p (i u) r -> p i r u", u=2),
            )
            free_banks.append(b)

        def turn_x(pr, g):
            turn(("x", pr, g), x_raw[pr], g)

        def gather_x(pr, g):
            h = pr // 2
            if (h, g) not in xt:
                xt[h, g] = kept("xt%d_%d" % (h, g), [P, 2, PAIR * PACK], BF16)
            gather(("x", pr, g), xt[h, g][:, pr % 2, :])

        def turn_gates(pr):
            turn(("g", pr), g_raw[pr], 0)

        def gather_gates(pr):
            gt[pr] = ring("gt", 4, [P, PAIR * PACK], BF16)
            gather(("g", pr), gt[pr][:])

        def quantize_x(pr, g):
            xq[pr, g] = ring("xq", 9, [P, PAIR], U32)
            xs[pr, g] = ring("xs", 9, [P, PAIR], U8)
            quantize(xq[pr, g][:], xs[pr, g][:], xt[pr // 2, g][:, pr % 2, :])

        def group_factor(name, g, part, engine):
            key = (name, g)
            raw = down_raw[g] if name == "down" else up_raw[g]
            if key not in grouped:
                grouped[key] = ring("grouped", 3, [P, KP * PACK], BF16)
            span = slice(0, 64) if part == 2 else slice(32 * part, 32 * (part + 1))
            dst = grouped[key][:].rearrange("p (t m i j) -> p m t i j", t=PACK, i=2, j=PACK)[:, span]
            src = raw[:].rearrange("p j (m i t) -> p m t i j", i=2, t=PACK)[:, span]
            if engine == "v":
                nc.vector.tensor_copy(out=dst, in_=src)
            else:
                nc.scalar.copy(out=dst, in_=src)

        def quantize_factor(name, g):
            key = (name, g)
            codes, scales = (dq, ds) if name == "down" else (uq, us)
            codes[key[1]] = kept("%s_q%d" % key, [P, KP], U32)
            scales[key[1]] = kept("%s_s%d" % key, [P, KP], U8)
            quantize(codes[key[1]][:], scales[key[1]][:], grouped[key][:])

        def order_w_codes(n, g):
            wq[n, g] = kept("wq%d_%d" % (n, g), [P, 2 * KP], U8)
            nc.vector.tensor_copy(
                out=wq[n, g][:].rearrange("p (t m b) -> p t m b", t=PACK, b=2),
                in_=w_raw[n][:, g, :].rearrange("p (m t b) -> p t m b", t=PACK, b=2),
            )

        def order_w_scales():
            nc.vector.tensor_copy(
                out=ws_rows[:].rearrange("p (n t m) -> p n t m", n=NG, t=PACK),
                in_=ws_raw[:].rearrange("p (n m t) -> p n t m", n=NG, t=PACK),
            )

        def stage1(i):
            pr = i // 2
            tok = slice((i % 2) * P, (i % 2 + 1) * P)
            held["z", i] = take_bank()
            bank = held["z", i][1]
            for t in range(PACK):
                col = slice(t * P, (t + 1) * P)
                for g in range(DG):
                    nc.tensor.matmul_mx(
                        out=bank[:, t, :], lhsT=dq[g][:, col].bitcast(FP8X4), lhsT_scale=ds[g][:, col],
                        rhs=xq[pr, g][:, tok].bitcast(FP8X4), rhs_scale=xs[pr, g][:, tok],
                        start=(g == 0), stop=(g == DG - 1),
                    )

        def gate(i):
            pr = i // 2
            b, bank = held["z", i]
            if pr not in hb:
                hb[pr] = ring("hb", 2, [P, PAIR * PACK], BF16)
            span = slice((i % 2) * KP, (i % 2 + 1) * KP)
            nc.vector.tensor_tensor(
                out=hb[pr][:, span].rearrange("p (r t) -> p r t", t=PACK),
                in0=bank[:].rearrange("p t r -> p r t"),
                in1=gt[pr][:, span].rearrange("p (r t) -> p r t", t=PACK),
                op=ALU.mult,
            )
            free_banks.append(b)

        def quantize_h(pr):
            hq[pr] = ring("hq", 2, [P, PAIR], U32)
            hs[pr] = ring("hs", 2, [P, PAIR], U8)
            quantize(hq[pr][:], hs[pr][:], hb[pr][:])

        def stage2(i, g):
            pr = i // 2
            tok = slice((i % 2) * P, (i % 2 + 1) * P)
            held["u", i, g] = take_bank()
            bank = held["u", i, g][1]
            for t in range(PACK):
                col = slice(t * P, (t + 1) * P)
                nc.tensor.matmul_mx(
                    out=bank[:, t, :], lhsT=uq[g][:, col].bitcast(FP8X4), lhsT_scale=us[g][:, col],
                    rhs=hq[pr][:, tok].bitcast(FP8X4), rhs_scale=hs[pr][:, tok], start=True, stop=True,
                )

        def correct(i, g):
            pr = i // 2
            b, bank = held["u", i, g]
            span = slice((i % 2) * KP, (i % 2 + 1) * KP)
            x_part = xt[i // 4, g][:, pr % 2, span].rearrange("p (r t) -> p r t", t=PACK)
            nc.vector.tensor_tensor(out=x_part, in0=bank[:].rearrange("p t r -> p r t"), in1=x_part, op=ALU.add)
            free_banks.append(b)

        def quantize_x1(h, g):
            x1q[h, g] = kept("x1q%d_%d" % (h, g), [P, HALF], U32)
            x1s[h, g] = kept("x1s%d_%d" % (h, g), [P, HALF], U8)
            quantize(x1q[h, g][:], x1s[h, g][:], xt[h, g][:].rearrange("p i c -> p (i c)"))

        yt, acc, yb = {}, {}, {}
        y_scales = [kept("y_scales%d" % h, [P, HALF], U8) for h in range(2)]

        def stage3_pass(k, t, g):
            h, n = divmod(k, NG)
            if g == 0:
                acc[k, t] = take_bank()
            nc.tensor.matmul_mx(
                out=acc[k, t][1][:].rearrange("p a b -> p (a b)"),
                lhsT=wq[n, g][:, 2 * P * t : 2 * P * (t + 1)].bitcast(FP4X4),
                lhsT_scale=ws[:, g, KP * n + P * t : KP * n + P * (t + 1)],
                rhs=x1q[h, g][:].bitcast(FP8X4), rhs_scale=x1s[h, g][:],
                start=(g == 0), stop=(g == DG - 1),
            )

        def silu(k, t):
            n = k % NG
            if k not in yt:
                yt[k] = wide([P, PACK, HALF], F32)
            b, bank = acc[k, t]
            nc.scalar.activation(
                out=yt[k][:, t, :], in_=bank[:].rearrange("p a b -> p (a b)"), func=ACT.Silu,
                bias=bias_sb[:, n, t : t + 1],
            )
            free_banks.append(b)

        def apply_gain(k, t, on):
            factor = gain_f32[:, k % NG, t : t + 1]
            if on == "v":
                nc.vector.tensor_scalar(
                    out=yt[k][:, t, :], in0=yt[k][:, t, :], scalar1=factor, scalar2=None, op0=ALU.mult
                )
            else:
                nc.scalar.activation(out=yt[k][:, t, :], in_=yt[k][:, t, :], func=ACT.Copy, scale=factor)

        def turn_y(k, i):
            held["y", k, i] = take_bank()
            bank = held["y", k, i][1]
            for t in range(PACK):
                nc.tensor.transpose(bank[:, t, :], yt[k][:, t, i * P : (i + 1) * P], ident[:])

        y_rows = {}

        def gather_y(k, i, on):
            b, bank = held["y", k, i]
            if (k, i // 2) not in y_rows:
                y_rows[k, i // 2] = ring("y_rows", 4, [P, 2, KP], F32)
            dst = y_rows[k, i // 2][:, i % 2, :].rearrange("r (p t) -> r p t", t=PACK)
            src = bank[:].rearrange("r t p -> r p t")
            if on == "v":
                nc.vector.tensor_copy(out=dst, in_=src)
            else:
                nc.scalar.copy(out=dst, in_=src)
            free_banks.append(b)

        def store_y(k, i0, i1):
            h, n = divmod(k, NG)
            rows = out_0[h * HALF + i0 * P : h * HALF + i1 * P, n * KP : (n + 1) * KP]
            src = y_rows[k, i0 // 2][:, i0 % 2 : i0 % 2 + i1 - i0, :]
            nc.sync.dma_start(out=rows.rearrange("(i p) n -> p i n", p=P), in_=src)

        y_codes = {}

        def group_y(k, part, engine):
            if k not in yb:
                yb[k] = ring("yb", 2, [P, HALF * PACK], BF16)
            span = slice(0, 128) if part == 2 else slice(64 * part, 64 * (part + 1))
            dst = yb[k][:].rearrange("p (c i t) -> p c t i", i=4, t=PACK)[:, span]
            src = yt[k][:].rearrange("p t (c i) -> p c t i", i=4)[:, span]
            if engine == "v":
                nc.vector.tensor_copy(out=dst, in_=src)
            else:
                nc.scalar.copy(out=dst, in_=src)

        def quantize_y(k):
            h, n = divmod(k, NG)
            y_codes[k] = ring("y_codes", 3, [P, HALF], U32)
            quantize(y_codes[k][:], y_scales[h][4 * n :, :], yb[k][:])

        def store_codes(k):
            h, n = divmod(k, NG)
            dst = out_1[n, :, h * HALF : (h + 1) * HALF, :].rearrange("p m t -> p (m t)")
            nc.sync.dma_start(out=dst.bitcast(I32), in_=y_codes[k][:].bitcast(I32))

        def store_y_scales(h):
            for q in range(4):
                dst = out_2[:, 4 * q : 4 * q + 4, h * HALF : (h + 1) * HALF]
                nc.sync.dma_start(out=dst.bitcast(I32), in_=y_scales[h][32 * q : 32 * q + 16, :].bitcast(I32))


        def widen_gain():
            nc.scalar.copy(out=gain_f32[:], in_=gain_sb[:])

        jobs = {
            "lx": load_x, "lg": load_gates, "ld": load_down, "lu": load_up, "lw": load_w, "ls": load_w_scales,
            "lv": load_vectors, "lr": load_raw_scales, "wg": widen_gain, "tx": turn_x, "cx": gather_x, "tg": turn_gates, "cg": gather_gates,
            "qx": quantize_x, "gf": group_factor, "qf": quantize_factor, "wc": order_w_codes, "ws": order_w_scales,
            "s1": stage1, "h": gate, "qh": quantize_h, "s2": stage2, "x1": correct, "q1": quantize_x1,
            "s3": stage3_pass, "si": silu, "ga": apply_gain, "ty": turn_y, "cy": gather_y, "sy": store_y,
            "gy": group_y, "qy": quantize_y, "sc": store_codes, "ss": store_y_scales,
        }
        for job in ORDER:
            jobs[job[0]](*job[1:])
